import numpy as np
import ml_dtypes


def mxq(x, axis, fmt="e4m3"):
    dtype, down = {"e4m3": (ml_dtypes.float8_e4m3fn, 7), "e5m2": (ml_dtypes.float8_e5m2, 14)}[fmt]
    v = np.moveaxis(np.asarray(x, np.float32).astype(ml_dtypes.bfloat16).astype(np.float64), axis, -1)
    blocks = v.reshape(v.shape[:-1] + (-1, 32))
    amax = np.abs(blocks).max(-1, keepdims=True)
    byte = np.maximum(np.where(amax > 0, np.frexp(amax)[1] - 1 + 127, 0) - down, 1)
    scale = np.exp2(byte - 127.0)
    codes = (blocks / scale).astype(np.float32).astype(dtype).astype(np.float64)
    return np.moveaxis((codes * scale).reshape(v.shape), -1, axis)


WIDE = False


def mx_kscale(k):
    if not WIDE:
        return np.ones(k)
    levels = np.array([30, -30])
    if k % 512:
        return np.exp2(np.random.permutation(np.resize(levels, k // 32))).repeat(32)
    a = np.empty((k // 512, 16))
    for p in range(k // 512):
        a[p, :8] = np.random.permutation(np.resize(levels, 8))
        for g in range(8):
            far = levels[np.abs(levels - a[p, g]) >= 10]
            a[p, g + 8] = far[np.random.randint(len(far))]
    return np.exp2(a.ravel()).repeat(32)


def f64(x):
    return np.asarray(x).astype(np.float64)


def striped(idx):
    return np.tile(np.asarray(idx).reshape(-1, 16).T, (8, 1)).astype(np.uint16)


def unstriped(offs):
    return offs[:16].T.reshape(-1).astype(np.int64)


E2M1 = np.array([0.0, 0.5, 1.0, 1.5, 2.0, 3.0, 4.0, 6.0, -0.0, -0.5, -1.0, -1.5, -2.0, -3.0, -4.0, -6.0])


def pack_weight(w, fmt):
    k, n = w.shape
    w = f64(np.asarray(w, np.float32).astype(ml_dtypes.bfloat16)).reshape(k // 32, 32, n)
    amax = np.abs(w).max(1)
    if fmt == "e4m3":
        byte = np.frexp(amax)[1] - 1 + 127 - 7
    else:
        mant, ex = np.frexp(amax / 6.0)
        byte = np.where(mant > 0.5, ex, ex - 1) + 127
    byte = np.clip(np.where(amax > 0, byte, 1), 1, 254)
    scaled = (w * np.exp2(127.0 - byte)[:, None, :]).reshape(k, n).astype(np.float32)
    by_word = np.ascontiguousarray(scaled.reshape(k // 512, 128, 4, n).transpose(0, 1, 3, 2))
    if fmt == "e4m3":
        words = by_word.astype(ml_dtypes.float8_e4m3fn).view(np.uint8)
    else:
        c = by_word.astype(ml_dtypes.float4_e2m1fn).view(np.uint8) & 0xF
        words = (c[..., 0::2] | (c[..., 1::2] << 4)).reshape(k // 512, 128, 2 * n)
    return np.ascontiguousarray(words), np.ascontiguousarray(byte.astype(np.uint8).reshape(k // 512, 16, n))


def unpack_weight(words, scales, fmt):
    g, _, n = scales.shape
    words = np.ascontiguousarray(words).reshape(g, 128, n, -1)
    if fmt == "e4m3":
        vals = words.view(ml_dtypes.float8_e4m3fn).astype(np.float64)
    else:
        nib = np.empty((g, 128, n, 4), np.uint8)
        nib[..., 0::2] = words & 0xF
        nib[..., 1::2] = words >> 4
        vals = E2M1[nib]
    vals = vals * np.repeat(np.exp2(scales.astype(np.float64) - 127.0), 8, axis=1)[..., None]
    return vals.transpose(0, 1, 3, 2).reshape(g * 512, n)


def bf(x):
    return np.asarray(x, np.float32).astype(ml_dtypes.bfloat16)


def planes(Y):
    r, m = Y.shape
    b = f64(bf(Y)).reshape(r // 32, 32, m)
    amax = np.abs(b).max(1)
    byte = np.clip(np.where(amax > 0, np.frexp(amax)[1] - 1 + 127 - 7, 1), 1, 254)
    codes = (b * np.exp2(127.0 - byte)[:, None, :]).reshape(r, m).astype(np.float32).astype(ml_dtypes.float8_e4m3fn).view(np.uint8)
    words = codes.reshape(r // 512, 128, 4, m).transpose(0, 1, 3, 2)
    return np.ascontiguousarray(words), np.ascontiguousarray(byte.astype(np.uint8).reshape(r // 512, 16, m))


K, R, N, T, J = 512, 512, 512, 1024, 512


def setup_inputs():
    n = np.random.standard_normal
    idx = np.random.permutation(T)[:J]
    fn = mx_kscale(N)
    fr = mx_kscale(R)
    wdp = pack_weight(n((N, R)) * 1 / np.sqrt(N) * fn[:, None], "e2m1")
    wup = pack_weight(n((R, K)) * 1 / np.sqrt(R) / fr[:, None], "e4m3")
    return {
        "g": (n((N, T)) * np.exp(0.5 * n((1, T))) / fn[:, None]).astype(np.float32),
        "wd_words": wdp[0],
        "wd_scales": wdp[1],
        "us": (np.random.uniform(0.5, 2.0, (R, 1)) * fr[:, None]).astype(np.float32),
        "wu_words": wup[0],
        "wu_scales": wup[1],
        "offs": striped(idx),
    }


def reference(g, wd_words, wd_scales, us, wu_words, wu_scales, offs):
    idx = unstriped(offs)
    wdu = unpack_weight(wd_words, wd_scales, "e2m1")
    wuu = unpack_weight(wu_words, wu_scales, "e4m3")
    gidxq = mxq(f64(g)[:, idx], 0, "e5m2")
    dh = wdu.T @ gidxq
    dc = np.maximum(np.minimum(dh, 1.0), 0.0 - 1.0) * f64(us)
    dcq = mxq(dc, 0, "e5m2")
    y = wuu.T @ dcq
    words, scales = planes(y)
    return y, words, scales

@@ -1,0 +1,170 @@
+from contextlib import ExitStack
+
+import concourse.mybir as mybir
+
+K, R, N, T, J = 512, 512, 512, 1024, 512
+FLOPS = 2 * J * (N * R + R * K)
+
+F32 = mybir.dt.float32
+BF16 = mybir.dt.bfloat16
+I32 = mybir.dt.int32
+U32 = mybir.dt.uint32
+U16 = mybir.dt.uint16
+U8 = mybir.dt.uint8
+E2M1X4 = mybir.dt.float4_e2m1fn_x4
+E4M3X4 = mybir.dt.float8_e4m3fn_x4
+E5M2X4 = mybir.dt.float8_e5m2_x4
+ACT = mybir.ActivationFunctionType
+ALU = mybir.AluOpType
+
+P = 128
+PACK = 4
+HALF = J // 2
+VECTOR_COLS = 352
+
+
+def deal(nc, dst, src, run):
+    nc.vector.tensor_copy(
+        out=dst.rearrange("p (t c i) -> p c t i", t=PACK, i=run),
+        in_=src.rearrange("p (c i t) -> p c t i", t=PACK, i=run),
+    )
+
+
+def weave(copy, halves, planes, j0, j1):
+    h = j0 // HALF
+    copy(
+        out=halves[h][:, j0 - h * HALF : j1 - h * HALF, :].rearrange("p (c i) t -> p c t i", i=4),
+        in_=planes[:, :, j0:j1].rearrange("p t (c i) -> p c t i", i=4),
+    )
+
+
+def weave_all(nc, halves, planes):
+    weave(nc.vector.tensor_copy, halves, planes, 0, HALF)
+    weave(nc.scalar.copy, halves, planes, VECTOR_COLS, J)
+    weave(nc.vector.tensor_copy, halves, planes, HALF, VECTOR_COLS)
+
+
+def quantise_half(nc, h, halves, codes, scales, fmt):
+    cols = slice(h * HALF, (h + 1) * HALF)
+    nc.vector.quantize_mx(
+        out=codes[:, cols].bitcast(fmt),
+        scales=scales[:, cols],
+        in_=halves[h][:].rearrange("p j t -> p (j t)"),
+    )
+
+
+def tile_list_clipped_back_pl_kernel(tc, g, wd_words, wd_scales, us, wu_words, wu_scales, offs, out_0, out_1, out_2):
+    nc = tc.nc
+    with ExitStack() as ctx:
+        keep = ctx.enter_context(tc.tile_pool(name="keep", bufs=1))
+        psum = ctx.enter_context(tc.psum_pool(name="psum", bufs=1))
+
+        offsets = keep.tile([P, J // 16], U16, name="offsets")
+        nc.sync.dma_start(offsets[:], offs)
+
+        raw_scales = keep.tile([P, 2 * R], U8, name="raw_scales", align_bytes=64)
+        nc.vector.memset(raw_scales[:].bitcast(I32), 0)
+
+        wd_raw = keep.tile([P, 2 * R], U8, name="wd_raw", align_bytes=64)
+        nc.sync.dma_start(wd_raw[:].bitcast(I32), wd_words[0].bitcast(I32))
+        for q in range(4):
+            nc.scalar.dma_start(
+                raw_scales[32 * q : 32 * q + 4, 0:R].bitcast(I32), wd_scales[0, 4 * q : 4 * q + 4, :].bitcast(I32)
+            )
+
+        g_rows = g.rearrange("(p t) c -> p t c", t=PACK)
+        windows = []
+        for t in range(PACK):
+            window = keep.tile([P, T], F32, name=f"window{t}", align_bytes=64)
+            nc.sync.dma_start(window[:], g_rows[:, t, :])
+            windows.append(window)
+
+        us_sb = keep.tile([P, PACK], F32, name="us_sb")
+        nc.scalar.dma_start(us_sb[:], us.rearrange("(p t) o -> p (t o)", t=PACK))
+        wu_raw = keep.tile([P, K], U32, name="wu_raw", align_bytes=64)
+        nc.sync.dma_start(wu_raw[:].bitcast(I32), wu_words[0].rearrange("p c r -> p (c r)").bitcast(I32))
+        for q in range(4):
+            nc.scalar.dma_start(
+                raw_scales[32 * q : 32 * q + 4, R : R + K].bitcast(I32), wu_scales[0, 4 * q : 4 * q + 4, :].bitcast(I32)
+            )
+
+        upper = keep.tile([P, PACK], F32, name="upper")
+        lower = keep.tile([P, PACK], F32, name="lower")
+        nc.scalar.activation(upper[:], us_sb[:], ACT.Abs)
+        nc.scalar.activation(lower[:], upper[:], ACT.Copy, scale=-1.0)
+
+        wd_codes = keep.tile([P, 2 * R], U8, name="wd_codes", align_bytes=64)
+        wd_plane = keep.tile([P, R], U8, name="wd_plane", align_bytes=64)
+        deal(nc, wd_codes[:].bitcast(U16), wd_raw[:].bitcast(U16), 8)
+        deal(nc, wd_plane[:], raw_scales[:, 0:R], 16)
+
+        picked = keep.tile([P, PACK, J], BF16, name="picked", align_bytes=64)
+        for t in range(PACK):
+            nc.vector.tensor_copy(picked[:, t, :], windows[t][:].indirect(offsets[:]))
+
+        g_halves = [keep.tile([P, HALF, PACK], BF16, name=f"g_half{h}", tag=f"g_half{h}", align_bytes=64) for h in range(2)]
+        weave_all(nc, g_halves, picked)
+        g_codes = keep.tile([P, J], U32, name="g_codes", align_bytes=64)
+        g_plane = keep.tile([P, J], U8, name="g_plane", align_bytes=64)
+        for h in range(2):
+            quantise_half(nc, h, g_halves, g_codes, g_plane, E5M2X4)
+
+        wu_dealt = keep.tile([P, 5 * K], U8, name="wu_dealt", tag="g_half1", align_bytes=64)
+        wu_codes = wu_dealt[:, 0 : 4 * K].bitcast(U32)
+        wu_plane = wu_dealt[:, 4 * K : 5 * K]
+        deal(nc, wu_codes, wu_raw[:], 4)
+        deal(nc, wu_plane, raw_scales[:, R : R + K], 16)
+
+        scaled = keep.tile([P, PACK, J], F32, name="scaled", align_bytes=64)
+        clipped = keep.tile([P, PACK, J], BF16, name="clipped", align_bytes=64)
+        for t in range(PACK):
+            dh = psum.tile([P, J], F32, name=f"dh{t}")
+            nc.tensor.matmul_mx(
+                out=dh[:],
+                lhsT=wd_codes[:, 2 * P * t : 2 * P * (t + 1)].bitcast(E2M1X4),
+                lhsT_scale=wd_plane[:, P * t : P * (t + 1)],
+                rhs=g_codes[:].bitcast(E5M2X4),
+                rhs_scale=g_plane[:],
+                start=True,
+                stop=True,
+            )
+            nc.scalar.activation(scaled[:, t, :], dh[:], ACT.Copy, scale=us_sb[:, t : t + 1])
+            nc.vector.tensor_scalar(
+                clipped[:, t, :], scaled[:, t, :], lower[:, t : t + 1], upper[:, t : t + 1], ALU.max, ALU.min
+            )
+
+        dc_halves = [keep.tile([P, HALF, PACK], BF16, name=f"dc_half{h}", align_bytes=64) for h in range(2)]
+        weave_all(nc, dc_halves, clipped)
+        dc_codes = keep.tile([P, J], U32, name="dc_codes", align_bytes=64)
+        dc_plane = keep.tile([P, J], U8, name="dc_plane", align_bytes=64)
+        for h in range(2):
+            quantise_half(nc, h, dc_halves, dc_codes, dc_plane, E5M2X4)
+
+        y = keep.tile([P, PACK, J], F32, name="y", align_bytes=64)
+        y_rows = out_0.rearrange("(p t) j -> p t j", t=PACK)
+        for t in range(PACK):
+            acc = psum.tile([P, J], F32, name=f"acc{t}")
+            nc.tensor.matmul_mx(
+                out=acc[:],
+                lhsT=wu_codes[:, P * t : P * (t + 1)].bitcast(E4M3X4),
+                lhsT_scale=wu_plane[:, P * t : P * (t + 1)],
+                rhs=dc_codes[:].bitcast(E5M2X4),
+                rhs_scale=dc_plane[:],
+                start=True,
+                stop=True,
+            )
+            nc.scalar.copy(y[:, t, :], acc[:])
+            nc.sync.dma_start(y_rows[:, t, :], y[:, t, :])
+
+        y_halves = [keep.tile([P, HALF, PACK], BF16, name=f"y_half{h}", align_bytes=64) for h in range(2)]
+        weave_all(nc, y_halves, y)
+        y_codes = keep.tile([P, J], U32, name="y_codes", align_bytes=64)
+        y_plane = keep.tile([P, J], U8, name="y_plane", align_bytes=64)
+        words = out_1[0].rearrange("p c r -> p (c r)").bitcast(I32)
+        for h in range(2):
+            quantise_half(nc, h, y_halves, y_codes, y_plane, E4M3X4)
+            cols = slice(h * HALF, (h + 1) * HALF)
+            nc.sync.dma_start(words[:, cols], y_codes[:, cols].bitcast(I32))
+        for q in range(4):
+            queue = nc.scalar if q % 2 == 0 else nc.sync
+            queue.dma_start(out_2[0, 4 * q : 4 * q + 4, :].bitcast(I32), y_plane[32 * q : 32 * q + 4, :].bitcast(I32))

@@ -20,7 +20,8 @@ ALU = mybir.AluOpType
 P = 128
 PACK = 4
 HALF = J // 2
-VECTOR_COLS = 352
+STEPPED = 192
+Y_VECTOR_COLS = 48
 
 
 def deal(nc, dst, src, run):
@@ -30,18 +31,12 @@ def deal(nc, dst, src, run):
     )
 
 
-def weave(copy, halves, planes, j0, j1):
-    h = j0 // HALF
-    copy(
-        out=halves[h][:, j0 - h * HALF : j1 - h * HALF, :].rearrange("p (c i) t -> p c t i", i=4),
-        in_=planes[:, :, j0:j1].rearrange("p t (c i) -> p c t i", i=4),
-    )
+def weave(copy, dst, planes):
+    copy(out=dst.rearrange("p (c i) t -> p c t i", i=4), in_=planes.rearrange("p t (c i) -> p c t i", i=4))
 
 
-def weave_all(nc, halves, planes):
-    weave(nc.vector.tensor_copy, halves, planes, 0, HALF)
-    weave(nc.scalar.copy, halves, planes, VECTOR_COLS, J)
-    weave(nc.vector.tensor_copy, halves, planes, HALF, VECTOR_COLS)
+def weave_pair(copy, dst, pair, u):
+    copy(out=dst[:, :, 2 * u : 2 * u + 2], in_=pair.rearrange("p e j -> p j e"))
 
 
 def quantise_half(nc, h, halves, codes, scales, fmt):
@@ -62,20 +57,20 @@ def tile_list_clipped_back_pl_kernel(tc, g, wd_words, wd_scales, us, wu_words, w
         offsets = keep.tile([P, J // 16], U16, name="offsets")
         nc.sync.dma_start(offsets[:], offs)
 
-        raw_scales = keep.tile([P, 2 * R], U8, name="raw_scales", align_bytes=64)
+        raw_scales = keep.tile([P, R], U8, name="raw_scales", align_bytes=64)
         nc.vector.memset(raw_scales[:].bitcast(I32), 0)
 
         wd_raw = keep.tile([P, 2 * R], U8, name="wd_raw", align_bytes=64)
         nc.sync.dma_start(wd_raw[:].bitcast(I32), wd_words[0].bitcast(I32))
         for q in range(4):
             nc.scalar.dma_start(
-                raw_scales[32 * q : 32 * q + 4, 0:R].bitcast(I32), wd_scales[0, 4 * q : 4 * q + 4, :].bitcast(I32)
+                raw_scales[32 * q : 32 * q + 4, :].bitcast(I32), wd_scales[0, 4 * q : 4 * q + 4, :].bitcast(I32)
             )
 
         g_rows = g.rearrange("(p t) c -> p t c", t=PACK)
         windows = []
         for t in range(PACK):
-            window = keep.tile([P, T], F32, name=f"window{t}", align_bytes=64)
+            window = keep.tile([P, T], F32, name=f"window{t}", tag=f"window{t}", align_bytes=64)
             nc.sync.dma_start(window[:], g_rows[:, t, :])
             windows.append(window)
 
@@ -83,10 +78,6 @@ def tile_list_clipped_back_pl_kernel(tc, g, wd_words, wd_scales, us, wu_words, w
         nc.scalar.dma_start(us_sb[:], us.rearrange("(p t) o -> p (t o)", t=PACK))
         wu_raw = keep.tile([P, K], U32, name="wu_raw", align_bytes=64)
         nc.sync.dma_start(wu_raw[:].bitcast(I32), wu_words[0].rearrange("p c r -> p (c r)").bitcast(I32))
-        for q in range(4):
-            nc.scalar.dma_start(
-                raw_scales[32 * q : 32 * q + 4, R : R + K].bitcast(I32), wu_scales[0, 4 * q : 4 * q + 4, :].bitcast(I32)
-            )
 
         upper = keep.tile([P, PACK], F32, name="upper")
         lower = keep.tile([P, PACK], F32, name="lower")
@@ -94,31 +85,43 @@ def tile_list_clipped_back_pl_kernel(tc, g, wd_words, wd_scales, us, wu_words, w
         nc.scalar.activation(lower[:], upper[:], ACT.Copy, scale=-1.0)
 
         wd_codes = keep.tile([P, 2 * R], U8, name="wd_codes", align_bytes=64)
-        wd_plane = keep.tile([P, R], U8, name="wd_plane", align_bytes=64)
         deal(nc, wd_codes[:].bitcast(U16), wd_raw[:].bitcast(U16), 8)
-        deal(nc, wd_plane[:], raw_scales[:, 0:R], 16)
+        for q in range(4):
+            nc.sync.dma_start(
+                wd_raw[32 * q : 32 * q + 4, 0:K].bitcast(I32), wu_scales[0, 4 * q : 4 * q + 4, :].bitcast(I32)
+            )
 
-        picked = keep.tile([P, PACK, J], BF16, name="picked", align_bytes=64)
-        for t in range(PACK):
-            nc.vector.tensor_copy(picked[:, t, :], windows[t][:].indirect(offsets[:]))
+        lists = [offsets[:, h * HALF // 16 : (h + 1) * HALF // 16] for h in range(2)]
+        low = keep.tile([P, 2, J], BF16, name="low", align_bytes=64)
+        high = [keep.tile([P, 2, HALF], BF16, name=f"high{h}", align_bytes=64) for h in range(2)]
+        g_halves = [
+            keep.tile([P, HALF, PACK], BF16, name=f"g_half{h}", tag=f"g_half{h}", align_bytes=64) for h in range(2)
+        ]
+        for t in range(2):
+            nc.vector.tensor_copy(low[:, t, :], windows[t][:].indirect(offsets[:]))
+        for h in range(2):
+            weave_pair(nc.scalar.copy, g_halves[h][:], low[:, :, h * HALF : (h + 1) * HALF], 0)
+        for t in range(2):
+            for h in (1, 0):
+                nc.vector.tensor_copy(high[h][:, t, :], windows[2 + t][:].indirect(lists[h]))
+        weave_pair(nc.scalar.copy, g_halves[1][:], high[1][:], 1)
+        wd_plane = keep.tile([P, R], U8, name="wd_plane", tag="window3", align_bytes=64)
+        deal(nc, wd_plane[:], raw_scales[:], 16)
+        weave_pair(nc.vector.tensor_copy, g_halves[0][:], high[0][:], 1)
 
-        g_halves = [keep.tile([P, HALF, PACK], BF16, name=f"g_half{h}", tag=f"g_half{h}", align_bytes=64) for h in range(2)]
-        weave_all(nc, g_halves, picked)
         g_codes = keep.tile([P, J], U32, name="g_codes", align_bytes=64)
         g_plane = keep.tile([P, J], U8, name="g_plane", align_bytes=64)
-        for h in range(2):
+        for h in (1, 0):
             quantise_half(nc, h, g_halves, g_codes, g_plane, E5M2X4)
 
-        wu_dealt = keep.tile([P, 5 * K], U8, name="wu_dealt", tag="g_half1", align_bytes=64)
+        wu_dealt = keep.tile([P, 5 * K], U8, name="wu_dealt", tag="g_half0", align_bytes=64)
         wu_codes = wu_dealt[:, 0 : 4 * K].bitcast(U32)
         wu_plane = wu_dealt[:, 4 * K : 5 * K]
         deal(nc, wu_codes, wu_raw[:], 4)
-        deal(nc, wu_plane, raw_scales[:, R : R + K], 16)
+        deal(nc, wu_plane, wd_raw[:, 0:K], 16)
 
-        scaled = keep.tile([P, PACK, J], F32, name="scaled", align_bytes=64)
-        clipped = keep.tile([P, PACK, J], BF16, name="clipped", align_bytes=64)
-        for t in range(PACK):
-            dh = psum.tile([P, J], F32, name=f"dh{t}")
+        def first_product(t, name):
+            dh = psum.tile([P, J], F32, name=name, tag=f"dh{t}")
             nc.tensor.matmul_mx(
                 out=dh[:],
                 lhsT=wd_codes[:, 2 * P * t : 2 * P * (t + 1)].bitcast(E2M1X4),
@@ -128,13 +131,22 @@ def tile_list_clipped_back_pl_kernel(tc, g, wd_words, wd_scales, us, wu_words, w
                 start=True,
                 stop=True,
             )
-            nc.scalar.activation(scaled[:, t, :], dh[:], ACT.Copy, scale=us_sb[:, t : t + 1])
-            nc.vector.tensor_scalar(
-                clipped[:, t, :], scaled[:, t, :], lower[:, t : t + 1], upper[:, t : t + 1], ALU.max, ALU.min
-            )
+            return dh
 
         dc_halves = [keep.tile([P, HALF, PACK], BF16, name=f"dc_half{h}", align_bytes=64) for h in range(2)]
-        weave_all(nc, dc_halves, clipped)
+        clipped = keep.tile([P, PACK, J - STEPPED], BF16, name="clipped", align_bytes=64)
+        for t in range(PACK):
+            dh = first_product(t, f"dh{t}")
+            scaled = keep.tile([P, J], F32, name=f"scaled{t}", align_bytes=64)
+            parts = [slice(0, J)] if t < PACK - 1 else [slice(STEPPED, J), slice(0, STEPPED)]
+            for cols in parts:
+                nc.scalar.activation(scaled[:, cols], dh[:, cols], ACT.Copy, scale=us_sb[:, t : t + 1])
+            for dst, cols in ((clipped[:, t, :], slice(STEPPED, J)), (dc_halves[0][:, :STEPPED, t], slice(0, STEPPED))):
+                nc.vector.tensor_scalar(dst, scaled[:, cols], lower[:, t : t + 1], upper[:, t : t + 1], ALU.max, ALU.min)
+        for n in range(2):
+            first_product(PACK - 1, f"warm{n}")
+        weave(nc.scalar.copy, dc_halves[1][:], clipped[:, :, HALF - STEPPED :])
+        weave(nc.vector.tensor_copy, dc_halves[0][:, STEPPED:, :], clipped[:, :, : HALF - STEPPED])
         dc_codes = keep.tile([P, J], U32, name="dc_codes", align_bytes=64)
         dc_plane = keep.tile([P, J], U8, name="dc_plane", align_bytes=64)
         for h in range(2):
@@ -153,11 +165,22 @@ def tile_list_clipped_back_pl_kernel(tc, g, wd_words, wd_scales, us, wu_words, w
                 start=True,
                 stop=True,
             )
-            nc.scalar.copy(y[:, t, :], acc[:])
-            nc.sync.dma_start(y_rows[:, t, :], y[:, t, :])
+            if t == 0:
+                for h in range(2):
+                    cols = slice(h * HALF, (h + 1) * HALF)
+                    nc.vector.tensor_copy(y[:, t, cols], acc[:, cols])
+                    nc.sync.dma_start(y_rows[:, t, cols], y[:, t, cols])
+                continue
+            (nc.vector.tensor_copy if t % 2 == 0 else nc.scalar.copy)(y[:, t, :], acc[:])
+            if t != 2:
+                rows = slice(min(t, 2), t + 1)
+                nc.sync.dma_start(y_rows[:, rows, :], y[:, rows, :])
 
         y_halves = [keep.tile([P, HALF, PACK], BF16, name=f"y_half{h}", align_bytes=64) for h in range(2)]
-        weave_all(nc, y_halves, y)
+        split = HALF + Y_VECTOR_COLS
+        weave(nc.vector.tensor_copy, y_halves[0][:], y[:, :, :HALF])
+        weave(nc.scalar.copy, y_halves[1][:, Y_VECTOR_COLS:, :], y[:, :, split:])
+        weave(nc.vector.tensor_copy, y_halves[1][:, :Y_VECTOR_COLS, :], y[:, :, HALF:split])
         y_codes = keep.tile([P, J], U32, name="y_codes", align_bytes=64)
         y_plane = keep.tile([P, J], U8, name="y_plane", align_bytes=64)
         words = out_1[0].rearrange("p c r -> p (c r)").bitcast(I32)
@@ -166,5 +189,4 @@ def tile_list_clipped_back_pl_kernel(tc, g, wd_words, wd_scales, us, wu_words, w
             cols = slice(h * HALF, (h + 1) * HALF)
             nc.sync.dma_start(words[:, cols], y_codes[:, cols].bitcast(I32))
         for q in range(4):
-            queue = nc.scalar if q % 2 == 0 else nc.sync
-            queue.dma_start(out_2[0, 4 * q : 4 * q + 4, :].bitcast(I32), y_plane[32 * q : 32 * q + 4, :].bitcast(I32))
+            nc.scalar.dma_start(out_2[0, 4 * q : 4 * q + 4, :].bitcast(I32), y_plane[32 * q : 32 * q + 4, :].bitcast(I32))

@@ -21,6 +21,7 @@ P = 128
 PACK = 4
 HALF = J // 2
 STEPPED = 192
+DC_VECTOR_COLS = 48
 Y_VECTOR_COLS = 48
 
 
@@ -91,9 +92,9 @@ def tile_list_clipped_back_pl_kernel(tc, g, wd_words, wd_scales, us, wu_words, w
                 wd_raw[32 * q : 32 * q + 4, 0:K].bitcast(I32), wu_scales[0, 4 * q : 4 * q + 4, :].bitcast(I32)
             )
 
-        lists = [offsets[:, h * HALF // 16 : (h + 1) * HALF // 16] for h in range(2)]
+        pieces = ((HALF, J), (HALF // 2, HALF), (0, HALF // 2))
         low = keep.tile([P, 2, J], BF16, name="low", align_bytes=64)
-        high = [keep.tile([P, 2, HALF], BF16, name=f"high{h}", align_bytes=64) for h in range(2)]
+        high = [keep.tile([P, 2, j1 - j0], BF16, name=f"high{j0}", align_bytes=64) for j0, j1 in pieces]
         g_halves = [
             keep.tile([P, HALF, PACK], BF16, name=f"g_half{h}", tag=f"g_half{h}", align_bytes=64) for h in range(2)
         ]
@@ -102,12 +103,13 @@ def tile_list_clipped_back_pl_kernel(tc, g, wd_words, wd_scales, us, wu_words, w
         for h in range(2):
             weave_pair(nc.scalar.copy, g_halves[h][:], low[:, :, h * HALF : (h + 1) * HALF], 0)
         for t in range(2):
-            for h in (1, 0):
-                nc.vector.tensor_copy(high[h][:, t, :], windows[2 + t][:].indirect(lists[h]))
-        weave_pair(nc.scalar.copy, g_halves[1][:], high[1][:], 1)
+            for n, (j0, j1) in enumerate(pieces):
+                nc.vector.tensor_copy(high[n][:, t, :], windows[2 + t][:].indirect(offsets[:, j0 // 16 : j1 // 16]))
+        weave_pair(nc.scalar.copy, g_halves[1][:], high[0][:], 1)
+        weave_pair(nc.scalar.copy, g_halves[0][:, HALF // 2 :, :], high[1][:], 1)
         wd_plane = keep.tile([P, R], U8, name="wd_plane", tag="window3", align_bytes=64)
         deal(nc, wd_plane[:], raw_scales[:], 16)
-        weave_pair(nc.vector.tensor_copy, g_halves[0][:], high[0][:], 1)
+        weave_pair(nc.vector.tensor_copy, g_halves[0][:, : HALF // 2, :], high[2][:], 1)
 
         g_codes = keep.tile([P, J], U32, name="g_codes", align_bytes=64)
         g_plane = keep.tile([P, J], U8, name="g_plane", align_bytes=64)
@@ -145,8 +147,10 @@ def tile_list_clipped_back_pl_kernel(tc, g, wd_words, wd_scales, us, wu_words, w
                 nc.vector.tensor_scalar(dst, scaled[:, cols], lower[:, t : t + 1], upper[:, t : t + 1], ALU.max, ALU.min)
         for n in range(2):
             first_product(PACK - 1, f"warm{n}")
-        weave(nc.scalar.copy, dc_halves[1][:], clipped[:, :, HALF - STEPPED :])
+        split = HALF + DC_VECTOR_COLS - STEPPED
+        weave(nc.scalar.copy, dc_halves[1][:, DC_VECTOR_COLS:, :], clipped[:, :, split:])
         weave(nc.vector.tensor_copy, dc_halves[0][:, STEPPED:, :], clipped[:, :, : HALF - STEPPED])
+        weave(nc.vector.tensor_copy, dc_halves[1][:, :DC_VECTOR_COLS, :], clipped[:, :, HALF - STEPPED : split])
         dc_codes = keep.tile([P, J], U32, name="dc_codes", align_bytes=64)
         dc_plane = keep.tile([P, J], U8, name="dc_plane", align_bytes=64)
         for h in range(2):
@@ -189,4 +193,5 @@ def tile_list_clipped_back_pl_kernel(tc, g, wd_words, wd_scales, us, wu_words, w
             cols = slice(h * HALF, (h + 1) * HALF)
             nc.sync.dma_start(words[:, cols], y_codes[:, cols].bitcast(I32))
         for q in range(4):
-            nc.scalar.dma_start(out_2[0, 4 * q : 4 * q + 4, :].bitcast(I32), y_plane[32 * q : 32 * q + 4, :].bitcast(I32))
+            queue = nc.scalar if q < 2 else nc.sync
+            queue.dma_start(out_2[0, 4 * q : 4 * q + 4, :].bitcast(I32), y_plane[32 * q : 32 * q + 4, :].bitcast(I32))

from contextlib import ExitStack

import concourse.mybir as mybir

K, R, N, T, J = 512, 512, 512, 1024, 512
FLOPS = 2 * J * (N * R + R * K)

F32 = mybir.dt.float32
BF16 = mybir.dt.bfloat16
I32 = mybir.dt.int32
U32 = mybir.dt.uint32
U16 = mybir.dt.uint16
U8 = mybir.dt.uint8
E2M1X4 = mybir.dt.float4_e2m1fn_x4
E4M3X4 = mybir.dt.float8_e4m3fn_x4
E5M2X4 = mybir.dt.float8_e5m2_x4
ACT = mybir.ActivationFunctionType
ALU = mybir.AluOpType

P = 128
PACK = 4
HALF = J // 2
STEPPED = 192
DC_VECTOR_COLS = 48
Y_VECTOR_COLS = 48


def deal(nc, dst, src, run):
    nc.vector.tensor_copy(
        out=dst.rearrange("p (t c i) -> p c t i", t=PACK, i=run),
        in_=src.rearrange("p (c i t) -> p c t i", t=PACK, i=run),
    )


def weave(copy, dst, planes):
    copy(out=dst.rearrange("p (c i) t -> p c t i", i=4), in_=planes.rearrange("p t (c i) -> p c t i", i=4))


def weave_pair(copy, dst, pair, u):
    copy(out=dst[:, :, 2 * u : 2 * u + 2], in_=pair.rearrange("p e j -> p j e"))


def quantise_half(nc, h, halves, codes, scales, fmt):
    cols = slice(h * HALF, (h + 1) * HALF)
    nc.vector.quantize_mx(
        out=codes[:, cols].bitcast(fmt),
        scales=scales[:, cols],
        in_=halves[h][:].rearrange("p j t -> p (j t)"),
    )


def tile_list_clipped_back_pl_kernel(tc, g, wd_words, wd_scales, us, wu_words, wu_scales, offs, out_0, out_1, out_2):
    nc = tc.nc
    with ExitStack() as ctx:
        keep = ctx.enter_context(tc.tile_pool(name="keep", bufs=1))
        psum = ctx.enter_context(tc.psum_pool(name="psum", bufs=1))

        offsets = keep.tile([P, J // 16], U16, name="offsets")
        nc.sync.dma_start(offsets[:], offs)

        raw_scales = keep.tile([P, R], U8, name="raw_scales", align_bytes=64)
        nc.vector.memset(raw_scales[:].bitcast(I32), 0)

        wd_raw = keep.tile([P, 2 * R], U8, name="wd_raw", align_bytes=64)
        nc.sync.dma_start(wd_raw[:].bitcast(I32), wd_words[0].bitcast(I32))
        for q in range(4):
            nc.scalar.dma_start(
                raw_scales[32 * q : 32 * q + 4, :].bitcast(I32), wd_scales[0, 4 * q : 4 * q + 4, :].bitcast(I32)
            )

        g_rows = g.rearrange("(p t) c -> p t c", t=PACK)
        windows = []
        for t in range(PACK):
            window = keep.tile([P, T], F32, name=f"window{t}", tag=f"window{t}", align_bytes=64)
            nc.sync.dma_start(window[:], g_rows[:, t, :])
            windows.append(window)

        us_sb = keep.tile([P, PACK], F32, name="us_sb")
        nc.scalar.dma_start(us_sb[:], us.rearrange("(p t) o -> p (t o)", t=PACK))
        wu_raw = keep.tile([P, K], U32, name="wu_raw", align_bytes=64)
        nc.sync.dma_start(wu_raw[:].bitcast(I32), wu_words[0].rearrange("p c r -> p (c r)").bitcast(I32))

        upper = keep.tile([P, PACK], F32, name="upper")
        lower = keep.tile([P, PACK], F32, name="lower")
        nc.scalar.activation(upper[:], us_sb[:], ACT.Abs)
        nc.scalar.activation(lower[:], upper[:], ACT.Copy, scale=-1.0)

        wd_codes = keep.tile([P, 2 * R], U8, name="wd_codes", align_bytes=64)
        deal(nc, wd_codes[:].bitcast(U16), wd_raw[:].bitcast(U16), 8)
        for q in range(4):
            nc.sync.dma_start(
                wd_raw[32 * q : 32 * q + 4, 0:K].bitcast(I32), wu_scales[0, 4 * q : 4 * q + 4, :].bitcast(I32)
            )

        pieces = ((HALF, J), (HALF // 2, HALF), (0, HALF // 2))
        low = keep.tile([P, 2, J], BF16, name="low", align_bytes=64)
        high = [keep.tile([P, 2, j1 - j0], BF16, name=f"high{j0}", align_bytes=64) for j0, j1 in pieces]
        g_halves = [
            keep.tile([P, HALF, PACK], BF16, name=f"g_half{h}", tag=f"g_half{h}", align_bytes=64) for h in range(2)
        ]
        for t in range(2):
            nc.vector.tensor_copy(low[:, t, :], windows[t][:].indirect(offsets[:]))
        for h in range(2):
            weave_pair(nc.scalar.copy, g_halves[h][:], low[:, :, h * HALF : (h + 1) * HALF], 0)
        for t in range(2):
            for n, (j0, j1) in enumerate(pieces):
                nc.vector.tensor_copy(high[n][:, t, :], windows[2 + t][:].indirect(offsets[:, j0 // 16 : j1 // 16]))
        weave_pair(nc.scalar.copy, g_halves[1][:], high[0][:], 1)
        weave_pair(nc.scalar.copy, g_halves[0][:, HALF // 2 :, :], high[1][:], 1)
        wd_plane = keep.tile([P, R], U8, name="wd_plane", tag="window3", align_bytes=64)
        deal(nc, wd_plane[:], raw_scales[:], 16)
        weave_pair(nc.vector.tensor_copy, g_halves[0][:, : HALF // 2, :], high[2][:], 1)

        g_codes = keep.tile([P, J], U32, name="g_codes", align_bytes=64)
        g_plane = keep.tile([P, J], U8, name="g_plane", align_bytes=64)
        for h in (1, 0):
            quantise_half(nc, h, g_halves, g_codes, g_plane, E5M2X4)

        wu_dealt = keep.tile([P, 5 * K], U8, name="wu_dealt", tag="g_half0", align_bytes=64)
        wu_codes = wu_dealt[:, 0 : 4 * K].bitcast(U32)
        wu_plane = wu_dealt[:, 4 * K : 5 * K]
        deal(nc, wu_codes, wu_raw[:], 4)
        deal(nc, wu_plane, wd_raw[:, 0:K], 16)

        def first_product(t, name):
            dh = psum.tile([P, J], F32, name=name, tag=f"dh{t}")
            nc.tensor.matmul_mx(
                out=dh[:],
                lhsT=wd_codes[:, 2 * P * t : 2 * P * (t + 1)].bitcast(E2M1X4),
                lhsT_scale=wd_plane[:, P * t : P * (t + 1)],
                rhs=g_codes[:].bitcast(E5M2X4),
                rhs_scale=g_plane[:],
                start=True,
                stop=True,
            )
            return dh

        dc_halves = [keep.tile([P, HALF, PACK], BF16, name=f"dc_half{h}", align_bytes=64) for h in range(2)]
        clipped = keep.tile([P, PACK, J - STEPPED], BF16, name="clipped", align_bytes=64)
        for t in range(PACK):
            dh = first_product(t, f"dh{t}")
            scaled = keep.tile([P, J], F32, name=f"scaled{t}", align_bytes=64)
            parts = [slice(0, J)] if t < PACK - 1 else [slice(STEPPED, J), slice(0, STEPPED)]
            for cols in parts:
                nc.scalar.activation(scaled[:, cols], dh[:, cols], ACT.Copy, scale=us_sb[:, t : t + 1])
            for dst, cols in ((clipped[:, t, :], slice(STEPPED, J)), (dc_halves[0][:, :STEPPED, t], slice(0, STEPPED))):
                nc.vector.tensor_scalar(dst, scaled[:, cols], lower[:, t : t + 1], upper[:, t : t + 1], ALU.max, ALU.min)
        for n in range(2):
            first_product(PACK - 1, f"warm{n}")
        split = HALF + DC_VECTOR_COLS - STEPPED
        weave(nc.scalar.copy, dc_halves[1][:, DC_VECTOR_COLS:, :], clipped[:, :, split:])
        weave(nc.vector.tensor_copy, dc_halves[0][:, STEPPED:, :], clipped[:, :, : HALF - STEPPED])
        weave(nc.vector.tensor_copy, dc_halves[1][:, :DC_VECTOR_COLS, :], clipped[:, :, HALF - STEPPED : split])
        dc_codes = keep.tile([P, J], U32, name="dc_codes", align_bytes=64)
        dc_plane = keep.tile([P, J], U8, name="dc_plane", align_bytes=64)
        for h in range(2):
            quantise_half(nc, h, dc_halves, dc_codes, dc_plane, E5M2X4)

        y = keep.tile([P, PACK, J], F32, name="y", align_bytes=64)
        y_rows = out_0.rearrange("(p t) j -> p t j", t=PACK)
        for t in range(PACK):
            acc = psum.tile([P, J], F32, name=f"acc{t}")
            nc.tensor.matmul_mx(
                out=acc[:],
                lhsT=wu_codes[:, P * t : P * (t + 1)].bitcast(E4M3X4),
                lhsT_scale=wu_plane[:, P * t : P * (t + 1)],
                rhs=dc_codes[:].bitcast(E5M2X4),
                rhs_scale=dc_plane[:],
                start=True,
                stop=True,
            )
            if t == 0:
                for h in range(2):
                    cols = slice(h * HALF, (h + 1) * HALF)
                    nc.vector.tensor_copy(y[:, t, cols], acc[:, cols])
                    nc.sync.dma_start(y_rows[:, t, cols], y[:, t, cols])
                continue
            (nc.vector.tensor_copy if t % 2 == 0 else nc.scalar.copy)(y[:, t, :], acc[:])
            if t != 2:
                rows = slice(min(t, 2), t + 1)
                nc.sync.dma_start(y_rows[:, rows, :], y[:, rows, :])

        y_halves = [keep.tile([P, HALF, PACK], BF16, name=f"y_half{h}", align_bytes=64) for h in range(2)]
        split = HALF + Y_VECTOR_COLS
        weave(nc.vector.tensor_copy, y_halves[0][:], y[:, :, :HALF])
        weave(nc.scalar.copy, y_halves[1][:, Y_VECTOR_COLS:, :], y[:, :, split:])
        weave(nc.vector.tensor_copy, y_halves[1][:, :Y_VECTOR_COLS, :], y[:, :, HALF:split])
        y_codes = keep.tile([P, J], U32, name="y_codes", align_bytes=64)
        y_plane = keep.tile([P, J], U8, name="y_plane", align_bytes=64)
        words = out_1[0].rearrange("p c r -> p (c r)").bitcast(I32)
        for h in range(2):
            quantise_half(nc, h, y_halves, y_codes, y_plane, E4M3X4)
            cols = slice(h * HALF, (h + 1) * HALF)
            nc.sync.dma_start(words[:, cols], y_codes[:, cols].bitcast(I32))
        for q in range(4):
            queue = nc.scalar if q < 2 else nc.sync
            queue.dma_start(out_2[0, 4 * q : 4 * q + 4, :].bitcast(I32), y_plane[32 * q : 32 * q + 4, :].bitcast(I32))
